import numpy as np
import ml_dtypes


def mxq(x, axis, fmt="e4m3"):
    dtype, down = {"e4m3": (ml_dtypes.float8_e4m3fn, 7), "e5m2": (ml_dtypes.float8_e5m2, 14)}[fmt]
    v = np.moveaxis(np.asarray(x, np.float32).astype(ml_dtypes.bfloat16).astype(np.float64), axis, -1)
    blocks = v.reshape(v.shape[:-1] + (-1, 32))
    amax = np.abs(blocks).max(-1, keepdims=True)
    byte = np.maximum(np.where(amax > 0, np.frexp(amax)[1] - 1 + 127, 0) - down, 1)
    scale = np.exp2(byte - 127.0)
    codes = (blocks / scale).astype(np.float32).astype(dtype).astype(np.float64)
    return np.moveaxis((codes * scale).reshape(v.shape), -1, axis)


WIDE = False


def mx_kscale(k):
    if not WIDE:
        return np.ones(k)
    levels = np.array([10, -10, 5, -5, 0])
    if k % 512:
        return np.exp2(np.random.permutation(np.resize(levels, k // 32))).repeat(32)
    a = np.empty((k // 512, 16))
    for p in range(k // 512):
        a[p, :8] = np.random.permutation(np.resize(levels, 8))
        for g in range(8):
            far = levels[np.abs(levels - a[p, g]) >= 10]
            a[p, g + 8] = far[np.random.randint(len(far))]
    return np.exp2(a.ravel()).repeat(32)


def f64(x):
    return np.asarray(x).astype(np.float64)


def striped(idx):
    return np.tile(idx.reshape(-1, 16).T, (8, 1)).astype(np.uint16)


def unstriped(offs):
    return offs[:16].T.reshape(-1).astype(np.int64)


E2M1 = np.array([0.0, 0.5, 1.0, 1.5, 2.0, 3.0, 4.0, 6.0, -0.0, -0.5, -1.0, -1.5, -2.0, -3.0, -4.0, -6.0])


def pack_weight(w, fmt):
    k, n = w.shape
    w = f64(np.asarray(w, np.float32).astype(ml_dtypes.bfloat16)).reshape(k // 32, 32, n)
    amax = np.abs(w).max(1)
    if fmt == "e4m3":
        byte = np.frexp(amax)[1] - 1 + 127 - 7
    else:
        mant, ex = np.frexp(amax / 6.0)
        byte = np.where(mant > 0.5, ex, ex - 1) + 127
    byte = np.clip(np.where(amax > 0, byte, 1), 1, 254)
    scaled = (w * np.exp2(127.0 - byte)[:, None, :]).reshape(k, n).astype(np.float32)
    by_word = np.ascontiguousarray(scaled.reshape(k // 512, 128, 4, n).transpose(0, 1, 3, 2))
    if fmt == "e4m3":
        words = by_word.astype(ml_dtypes.float8_e4m3fn).view(np.uint8)
    else:
        c = by_word.astype(ml_dtypes.float4_e2m1fn).view(np.uint8) & 0xF
        words = (c[..., 0::2] | (c[..., 1::2] << 4)).reshape(k // 512, 128, 2 * n)
    return np.ascontiguousarray(words), np.ascontiguousarray(byte.astype(np.uint8).reshape(k // 512, 16, n))


def unpack_weight(words, scales, fmt):
    g, _, n = scales.shape
    words = np.ascontiguousarray(words).reshape(g, 128, n, -1)
    if fmt == "e4m3":
        vals = words.view(ml_dtypes.float8_e4m3fn).astype(np.float64)
    else:
        nib = np.empty((g, 128, n, 4), np.uint8)
        nib[..., 0::2] = words & 0xF
        nib[..., 1::2] = words >> 4
        vals = E2M1[nib]
    vals = vals * np.repeat(np.exp2(scales.astype(np.float64) - 127.0), 8, axis=1)[..., None]
    return vals.transpose(0, 1, 3, 2).reshape(g * 512, n)


def gelu(v):
    return 0.5 * v * (1.0 + np.tanh(np.sqrt(2.0 / np.pi) * (v + 0.044715 * v**3)))


K, H, T, S, T3, S2 = 1024, 1024, 2048, 512, 1024, 512

def setup_inputs():
    n = np.random.standard_normal
    s = mx_kscale(K)[:, None]
    u = mx_kscale(H)[:, None]
    tab_words, tab_scales = pack_weight(n((K, T)) * s, "e4m3")
    tab2_words, tab2_scales = pack_weight(n((H, T3)) / np.sqrt(H) / u, "e4m3")
    tab3_words, tab3_scales = pack_weight(n((H, T3)) / np.sqrt(H) / u, "e4m3")
    w2_words, w2_scales = pack_weight(0.5 * n((K, H)) / np.sqrt(K) / s * u.T, "e2m1")
    return {
        "tab_words": tab_words, "tab_scales": tab_scales,
        "tab2_words": tab2_words, "tab2_scales": tab2_scales,
        "tab3_words": tab3_words, "tab3_scales": tab3_scales,
        "offs": striped(np.random.permutation(T)[:S]),
        "offs2": striped(np.random.permutation(T3)[:S2]),
        "offs3": striped(np.random.permutation(T3)[:S2]),
        "w1": (0.54 * n((K, H)) / np.sqrt(K) / s).astype(np.float32),
        "w2_words": w2_words, "w2_scales": w2_scales,
        "gain": (2.0 * np.exp(0.3 * n(H)) * u[:, 0]).astype(np.float32),
        "least": (0.6 * n(S2)).astype(np.float32),
    }

def reference(tab_words, tab_scales, tab2_words, tab2_scales, tab3_words, tab3_scales,
              offs, offs2, offs3, w1, w2_words, w2_scales, gain, least):
    v = unpack_weight(tab_words, tab_scales, "e4m3")[:, unstriped(offs)]
    v2 = unpack_weight(tab2_words, tab2_scales, "e4m3")[:, unstriped(offs2)]
    v3 = unpack_weight(tab3_words, tab3_scales, "e4m3")[:, unstriped(offs3)]
    w1q = mxq(f64(w1), 0, "e4m3")
    w2 = unpack_weight(w2_words, w2_scales, "e2m1")
    wave = f64(gain)[:, None] * np.sin(w1q.T @ v)
    h = wave + (w2.T @ v)
    hq = mxq(h, 0, "e4m3")
    e2 = v2.T @ hq
    e3 = v3.T @ hq
    return np.minimum(np.maximum(e2, f64(least)[:, None]), e3)

@@ -1,0 +1,342 @@
+import math
+from contextlib import ExitStack
+
+import concourse.mybir as mybir
+
+K, H, T, S, T3, S2 = 1024, 1024, 2048, 512, 1024, 512
+FLOPS = 2 * (2 * K * H * S + 2 * H * S2 * S)
+
+F32 = mybir.dt.float32
+BF16 = mybir.dt.bfloat16
+I32 = mybir.dt.int32
+U32 = mybir.dt.uint32
+U16 = mybir.dt.uint16
+U8 = mybir.dt.uint8
+E4M3 = mybir.dt.float8_e4m3fn_x4
+E2M1 = mybir.dt.float4_e2m1fn_x4
+ALU = mybir.AluOpType
+ACT = mybir.ActivationFunctionType
+
+P = 128
+PACK = 4
+PASS = P * PACK
+NPASS = 2
+HALF = S // 2
+TWO_PI = 2.0 * math.pi
+TURN_OFFSET = 1024.0
+TURNS_ON_VECTOR = (0, 1)
+
+
+def tile_list_workshop_offer_score_kernel(
+    tc, tab_words, tab_scales, tab2_words, tab2_scales, tab3_words, tab3_scales,
+    offs, offs2, offs3, w1, w2_words, w2_scales, gain, least, out,
+):
+    nc = tc.nc
+    with ExitStack() as ctx:
+        keep = ctx.enter_context(tc.tile_pool(name="keep", bufs=1))
+        work = ctx.enter_context(tc.tile_pool(name="work", bufs=3))
+        stage = ctx.enter_context(tc.tile_pool(name="stage", bufs=4))
+        psum = ctx.enter_context(tc.psum_pool(name="psum", bufs=8))
+
+        def held(shape, dtype, name):
+            return keep.tile(shape, dtype, name=name, align_bytes=64)
+
+        idx = keep.tile([P, S // 16], U16, name="idx")
+        idx2 = keep.tile([P, S2 // 16], U16, name="idx2")
+        idx3 = keep.tile([P, S2 // 16], U16, name="idx3")
+
+        v_sc = held([P, NPASS, T], U8, "v_sc")
+        v2_sc = held([P, T3], U8, "v2_sc")
+        v3_sc = held([P, T3], U8, "v3_sc")
+        nc.vector.memset(v_sc[:].bitcast(I32), 0)
+        nc.vector.memset(v3_sc[:].bitcast(I32), 0)
+        nc.vector.memset(v2_sc[:].bitcast(I32), 0)
+
+        nc.sync.dma_start(idx[:], offs)
+        nc.sync.dma_start(idx3[:], offs3)
+        nc.sync.dma_start(idx2[:], offs2)
+        for q in range(4):
+            nc.scalar.dma_start(
+                v_sc[32 * q : 32 * q + 4, :, :].bitcast(I32),
+                tab_scales.bitcast(I32)[:, 4 * q : 4 * q + 4, :].rearrange("a r t -> r a t"),
+            )
+        gain_sb = held([P, NPASS, PACK], F32, "gain_sb")
+        nc.gpsimd.dma_start(gain_sb[:], gain.rearrange("(b p t) -> p b t", b=NPASS, t=PACK))
+        for sc_tile, sc_dram in ((v3_sc, tab3_scales), (v2_sc, tab2_scales)):
+            for q in range(4):
+                nc.gpsimd.dma_start(
+                    sc_tile[32 * q : 32 * q + 8, :].bitcast(I32),
+                    sc_dram.bitcast(I32)[:, 4 * q : 4 * q + 4, :],
+                )
+        least_sb = held([P, S2 // P], F32, "least_sb")
+        with nc.allow_non_contiguous_dma(reason="one value of least for each partition"):
+            nc.gpsimd.dma_start(least_sb[:], least.rearrange("(mt p) -> p mt", p=P))
+
+        def staged(shape, dtype):
+            return stage.tile(shape, dtype, name="staged", align_bytes=64)
+
+        def load_w1(b, a):
+            raw = staged([P, PACK, PASS], F32)
+            rows = w1[a * PASS : (a + 1) * PASS, b * PASS : (b + 1) * PASS]
+            nc.sync.dma_start(raw[:], rows.rearrange("(p i) c -> p i c", i=PACK))
+            w1_raw[b, a] = raw
+
+        def load_v(a):
+            words = staged([P, T], U32)
+            nc.sync.dma_start(
+                words[:].bitcast(I32), tab_words[a].rearrange("p n i -> p (n i)").bitcast(I32)
+            )
+            v_words[a] = words
+
+        def load_both_passes(name, dram, width, dtype):
+            words = staged([P, NPASS, width], dtype)
+            nc.sync.dma_start(words[:].bitcast(I32), dram.bitcast(I32).rearrange("a p c -> p a c"))
+            packed[name] = words
+
+        def load_w2_scales():
+            raw = staged([P, NPASS, H], U8)
+            nc.vector.memset(raw[:].bitcast(I32), 0)
+            for q in range(4):
+                nc.scalar.dma_start(
+                    raw[32 * q : 32 * q + 4, :, :].bitcast(I32),
+                    w2_scales.bitcast(I32)[:, 4 * q : 4 * q + 4, :].rearrange("a r t -> r a t"),
+                )
+            packed["w2_scales"] = raw
+
+        w1_raw, v_words, packed = {}, {}, {}
+        load_w1(0, 0)
+        load_w1(0, 1)
+        load_v(0)
+        load_v(1)
+
+        w1_bf, w1_codes, w1_plane = {}, {}, {}
+
+        def cast_w1(b, a):
+            grouped = held([P, PACK, P, PACK], BF16, "w1_bf_%d_%d" % (b, a))
+            nc.scalar.copy(
+                out=grouped[:].rearrange("p t m i -> p m i t"),
+                in_=w1_raw[b, a][:].rearrange("p i (m t) -> p m i t", t=PACK),
+            )
+            w1_bf[b, a] = grouped
+
+        def quantize_w1(b, a):
+            codes = held([P, PASS], U32, "w1_codes_%d_%d" % (b, a))
+            plane = held([P, PASS], U8, "plane_%d_%d" % (b, a))
+            nc.vector.quantize_mx(
+                out=codes[:].bitcast(E4M3),
+                scales=plane[:],
+                in_=w1_bf[b, a][:].rearrange("p t m i -> p (t m i)"),
+            )
+            w1_codes[b, a], w1_plane[b, a] = codes, plane
+
+        w2_codes, w2_plane = {}, {}
+
+        def deal(b, raw, dtype, name):
+            dealt = held([P, NPASS, PASS], dtype, "%s_%d" % (name, b))
+            nc.vector.tensor_copy(
+                out=dealt[:].rearrange("p a (t m) -> p a t m", t=PACK),
+                in_=raw[:, :, b * PASS : (b + 1) * PASS].rearrange("p a (m t) -> p a t m", t=PACK),
+            )
+            return dealt
+
+        def deal_w2_codes(b):
+            w2_codes[b] = deal(b, packed["w2"], U16, "w2_codes")
+
+        def deal_w2_plane(b):
+            w2_plane[b] = deal(b, packed["w2_scales"], U8, "w2_plane")
+
+        def gather(dst, window, offsets):
+            nc.vector.tensor_copy(dst, window.indirect(offsets))
+
+        g_words = [held([P, S], U32, "g_words_%d" % a) for a in range(NPASS)]
+        g_plane = [held([P, S], U8, "g_plane_%d" % a) for a in range(NPASS)]
+        g2_words = [held([P, S2], U32, "g2_words_%d" % b) for b in range(NPASS)]
+        g3_words = [held([P, S2], U32, "g3_words_%d" % b) for b in range(NPASS)]
+        picked_plane = {}
+
+        def gather_plane(name, window, offsets, slot):
+            plane = held([P, S2], U8, slot)
+            gather(plane[:], window[:], offsets[:])
+            picked_plane[name] = plane
+
+        steps = [(b, jh, tp) for b in range(NPASS) for jh in range(2) for tp in range(2)]
+        angle_ps, plain_ps, reduced, wave, h_rows = {}, {}, {}, {}, {}
+        h_bf, h_codes, h_plane = {}, {}, {}
+
+        def products(i):
+            b, jh, tp = steps[i]
+            cols = slice(jh * HALF, (jh + 1) * HALF)
+            x = psum.tile([P, 2, HALF], F32, name="bank")
+            for a in range(NPASS):
+                for u in range(2):
+                    m = slice((2 * tp + u) * P, (2 * tp + u + 1) * P)
+                    nc.tensor.matmul_mx(
+                        out=x[:, u, :],
+                        lhsT=w1_codes[b, a][:, m].bitcast(E4M3), lhsT_scale=w1_plane[b, a][:, m],
+                        rhs=g_words[a][:, cols].bitcast(E4M3), rhs_scale=g_plane[a][:, cols],
+                        start=(a == 0 and u == 0), stop=(a == NPASS - 1 and u == 1),
+                    )
+            y = psum.tile([P, 2, HALF], F32, name="bank")
+            for u in range(2):
+                m = slice((2 * tp + u) * P, (2 * tp + u + 1) * P)
+                for a in range(NPASS):
+                    nc.tensor.matmul_mx(
+                        out=y[:, u, :],
+                        lhsT=w2_codes[b][:, a, m].bitcast(E2M1), lhsT_scale=w2_plane[b][:, a, m],
+                        rhs=g_words[a][:, cols].bitcast(E4M3), rhs_scale=g_plane[a][:, cols],
+                        start=(a == 0), stop=(a == NPASS - 1),
+                    )
+            angle_ps[i], plain_ps[i] = x, y
+
+        turns = {}
+
+        def count_turns(i):
+            x = angle_ps[i][:].rearrange("p u j -> p (u j)")
+            if i in TURNS_ON_VECTOR:
+                k = work.tile([P, 2 * HALF], I32, name="turns_i")
+                nc.vector.tensor_scalar(k[:], x, 1.0 / TWO_PI, None, ALU.mult)
+                turns[i] = k
+            else:
+                k = work.tile([P, 2 * HALF], U32, name="turns_u")
+                nc.scalar.activation(k[:], x, ACT.Copy, bias=TURN_OFFSET, scale=1.0 / TWO_PI)
+                back = work.tile([P, 2 * HALF], F32, name="back")
+                nc.scalar.activation(
+                    back[:], k[:], ACT.Copy, bias=TURN_OFFSET * TWO_PI, scale=-TWO_PI
+                )
+                turns[i] = back
+
+        def reduce_angle(i):
+            x = angle_ps[i][:].rearrange("p u j -> p (u j)")
+            y = work.tile([P, 2 * HALF], F32, name="reduced")
+            if i in TURNS_ON_VECTOR:
+                nc.vector.scalar_tensor_tensor(y[:], turns[i][:], -TWO_PI, x, ALU.mult, ALU.add)
+            else:
+                nc.vector.tensor_tensor(y[:], x, turns[i][:], ALU.add)
+            reduced[i] = y
+
+        def sine(i):
+            s = work.tile([P, 2, HALF], F32, name="wave")
+            nc.scalar.activation(s[:].rearrange("p u j -> p (u j)"), reduced[i][:], ACT.Sin)
+            wave[i] = s
+
+        def combine(i):
+            b, jh, tp = steps[i]
+            if tp == 0:
+                h_rows[b, jh] = held([P, PACK, HALF], BF16, "h_rows_%d_%d" % (b, jh))
+            for u in range(2):
+                t = 2 * tp + u
+                nc.vector.scalar_tensor_tensor(
+                    h_rows[b, jh][:, t, :], wave[i][:, u, :], gain_sb[:, b, t : t + 1],
+                    plain_ps[i][:, u, :], ALU.mult, ALU.add,
+                )
+
+        def weave_h(b, jh, on_vector):
+            grouped = held([P, HALF, PACK], BF16, "h_bf_%d_%d" % (b, jh))
+            dst = grouped[:].rearrange("p (c i) t -> p c t i", i=4)
+            src = h_rows[b, jh][:].rearrange("p t (c i) -> p c t i", i=4)
+            if on_vector:
+                nc.vector.tensor_copy(out=dst, in_=src)
+            else:
+                nc.scalar.copy(out=dst, in_=src)
+            h_bf[b, jh] = grouped
+
+        def quantize_h(b, jh):
+            codes = held([P, HALF], U32, "h_codes_%d_%d" % (b, jh))
+            plane = held([P, HALF], U8, "h_plane_%d_%d" % (b, jh))
+            nc.vector.quantize_mx(
+                out=codes[:].bitcast(E4M3), scales=plane[:],
+                in_=h_bf[b, jh][:].rearrange("p j t -> p (j t)"),
+            )
+            h_codes[b, jh], h_plane[b, jh] = codes, plane
+
+        score_ps = {}
+
+        def score_pass(jh, b):
+            for mp in range(2):
+                for name, words in (("e3", g3_words), ("e2", g2_words)):
+                    plane = picked_plane[name]
+                    if b == 0:
+                        score_ps[jh, mp, name] = psum.tile([P, 2, HALF], F32, name="bank")
+                    bank = score_ps[jh, mp, name]
+                    for u in range(2):
+                        m = slice((2 * mp + u) * P, (2 * mp + u + 1) * P)
+                        nc.tensor.matmul_mx(
+                            out=bank[:, u, :],
+                            lhsT=words[b][:, m].bitcast(E4M3), lhsT_scale=plane[4 * b : P, m],
+                            rhs=h_codes[b, jh][:].bitcast(E4M3), rhs_scale=h_plane[b, jh][:],
+                            start=(b == 0 and u == 0), stop=(b == NPASS - 1 and u == 1),
+                        )
+
+        out_view = out.rearrange("(mt p) j -> p mt j", p=P)
+
+        def finish(jh):
+            for mp in range(2):
+                limit = work.tile([P, 2, HALF], F32, name="limit")
+                nc.scalar.copy(out=limit[:], in_=score_ps[jh, mp, "e3"][:])
+                res = held([P, 2, HALF], F32, "res_%d_%d" % (jh, mp))
+                for u in range(2):
+                    mt = 2 * mp + u
+                    nc.vector.scalar_tensor_tensor(
+                        res[:, u, :], score_ps[jh, mp, "e2"][:, u, :], least_sb[:, mt : mt + 1],
+                        limit[:, u, :], ALU.max, ALU.min,
+                    )
+                nc.sync.dma_start(
+                    out_view[:, 2 * mp : 2 * mp + 2, jh * HALF : (jh + 1) * HALF], res[:]
+                )
+
+        for a in range(NPASS):
+            gather(g_plane[a][:], v_sc[:, a, :], idx[:])
+        cast_w1(0, 0)
+        cast_w1(0, 1)
+        load_w2_scales()
+        load_both_passes("w2", w2_words, H, U16)
+        quantize_w1(0, 0)
+        gather(g_words[0][:], v_words[0][:], idx[:])
+        load_w1(1, 0)
+        quantize_w1(0, 1)
+        for jh in range(2):
+            gather(g_words[1][:, jh * HALF : (jh + 1) * HALF], v_words[1][:],
+                   idx[:, jh * (HALF // 16) : (jh + 1) * (HALF // 16)])
+        load_w1(1, 1)
+        deal_w2_codes(0)
+        deal_w2_plane(0)
+        deal_w2_plane(1)
+        load_both_passes("v3", tab3_words.rearrange("a p n i -> a p (n i)"), T3, U32)
+        deal_w2_codes(1)
+        load_both_passes("v2", tab2_words.rearrange("a p n i -> a p (n i)"), T3, U32)
+
+        fill = {
+            0: [lambda: cast_w1(1, 0)],
+            1: [lambda: quantize_w1(1, 0), lambda: cast_w1(1, 1)],
+            2: [lambda: quantize_w1(1, 1), lambda: gather_plane("e3", v3_sc, idx3, "plane_0_1")],
+            3: [lambda: weave_h(0, 0, False)],
+            4: [lambda: gather(g3_words[0][:], packed["v3"][:, 0, :], idx3[:]), lambda: quantize_h(0, 0)],
+            5: [lambda: gather(g2_words[0][:], packed["v2"][:, 0, :], idx2[:]), lambda: weave_h(0, 1, False)],
+            6: [lambda: gather_plane("e2", v2_sc, idx2, "plane_1_1"), lambda: gather(g3_words[1][:], packed["v3"][:, 1, :], idx3[:]), lambda: quantize_h(0, 1)],
+            7: [lambda: gather(g2_words[1][:], packed["v2"][:, 1, :], idx2[:]), lambda: weave_h(1, 0, False)],
+        }
+        n = len(steps)
+        for i in range(4):
+            products(i)
+        count_turns(0)
+        for i in range(n):
+            reduce_angle(i)
+            if i + 1 < n:
+                count_turns(i + 1)
+            sine(i)
+            if i >= 1:
+                combine(i - 1)
+            for job in fill.get(i, []):
+                job()
+            if i >= 2 and i + 2 < n:
+                products(i + 2)
+        combine(n - 1)
+        quantize_h(1, 0)
+        score_pass(0, 0)
+        score_pass(0, 1)
+        weave_h(1, 1, True)
+        score_pass(1, 0)
+        finish(0)
+        quantize_h(1, 1)
+        score_pass(1, 1)
+        finish(1)

@@ -24,7 +24,7 @@ NPASS = 2
 HALF = S // 2
 TWO_PI = 2.0 * math.pi
 TURN_OFFSET = 1024.0
-TURNS_ON_VECTOR = (0, 1)
+TURNS_ON_VECTOR = (0, 1,)
 
 
 def tile_list_workshop_offer_score_kernel(
@@ -34,7 +34,7 @@ def tile_list_workshop_offer_score_kernel(
     nc = tc.nc
     with ExitStack() as ctx:
         keep = ctx.enter_context(tc.tile_pool(name="keep", bufs=1))
-        work = ctx.enter_context(tc.tile_pool(name="work", bufs=3))
+        work = ctx.enter_context(tc.tile_pool(name="work", bufs=4))
         stage = ctx.enter_context(tc.tile_pool(name="stage", bufs=4))
         psum = ctx.enter_context(tc.psum_pool(name="psum", bufs=8))
 
@@ -46,29 +46,25 @@ def tile_list_workshop_offer_score_kernel(
         idx3 = keep.tile([P, S2 // 16], U16, name="idx3")
 
         v_sc = held([P, NPASS, T], U8, "v_sc")
-        v2_sc = held([P, T3], U8, "v2_sc")
-        v3_sc = held([P, T3], U8, "v3_sc")
+        w2_sc = held([P, NPASS, H], U8, "w2_sc")
         nc.vector.memset(v_sc[:].bitcast(I32), 0)
-        nc.vector.memset(v3_sc[:].bitcast(I32), 0)
-        nc.vector.memset(v2_sc[:].bitcast(I32), 0)
+        nc.gpsimd.memset(w2_sc[:].bitcast(I32), 0)
 
+        def load_scale_rows(queue, plane, dram):
+            for q in range(4):
+                queue.dma_start(
+                    plane[32 * q : 32 * q + 4, :, :].bitcast(I32),
+                    dram.bitcast(I32)[:, 4 * q : 4 * q + 4, :].rearrange("a r t -> r a t"),
+                )
+
+        gain_sb = held([P, NPASS, PACK], F32, "gain_sb")
+        least_sb = held([P, S2 // P], F32, "least_sb")
         nc.sync.dma_start(idx[:], offs)
         nc.sync.dma_start(idx3[:], offs3)
         nc.sync.dma_start(idx2[:], offs2)
-        for q in range(4):
-            nc.scalar.dma_start(
-                v_sc[32 * q : 32 * q + 4, :, :].bitcast(I32),
-                tab_scales.bitcast(I32)[:, 4 * q : 4 * q + 4, :].rearrange("a r t -> r a t"),
-            )
-        gain_sb = held([P, NPASS, PACK], F32, "gain_sb")
+        load_scale_rows(nc.scalar, v_sc, tab_scales)
+        load_scale_rows(nc.gpsimd, w2_sc, w2_scales)
         nc.gpsimd.dma_start(gain_sb[:], gain.rearrange("(b p t) -> p b t", b=NPASS, t=PACK))
-        for sc_tile, sc_dram in ((v3_sc, tab3_scales), (v2_sc, tab2_scales)):
-            for q in range(4):
-                nc.gpsimd.dma_start(
-                    sc_tile[32 * q : 32 * q + 8, :].bitcast(I32),
-                    sc_dram.bitcast(I32)[:, 4 * q : 4 * q + 4, :],
-                )
-        least_sb = held([P, S2 // P], F32, "least_sb")
         with nc.allow_non_contiguous_dma(reason="one value of least for each partition"):
             nc.gpsimd.dma_start(least_sb[:], least.rearrange("(mt p) -> p mt", p=P))
 
@@ -93,21 +89,16 @@ def tile_list_workshop_offer_score_kernel(
             nc.sync.dma_start(words[:].bitcast(I32), dram.bitcast(I32).rearrange("a p c -> p a c"))
             packed[name] = words
 
-        def load_w2_scales():
-            raw = staged([P, NPASS, H], U8)
-            nc.vector.memset(raw[:].bitcast(I32), 0)
+        def load_packed_scales(name, dram, plane):
+            nc.gpsimd.memset(plane[:].bitcast(I32), 0)
             for q in range(4):
-                nc.scalar.dma_start(
-                    raw[32 * q : 32 * q + 4, :, :].bitcast(I32),
-                    w2_scales.bitcast(I32)[:, 4 * q : 4 * q + 4, :].rearrange("a r t -> r a t"),
+                nc.sync.dma_start(
+                    plane[32 * q : 32 * q + 8, :].bitcast(I32),
+                    dram.bitcast(I32)[:, 4 * q : 4 * q + 4, :],
                 )
-            packed["w2_scales"] = raw
+            packed[name] = plane
 
         w1_raw, v_words, packed = {}, {}, {}
-        load_w1(0, 0)
-        load_w1(0, 1)
-        load_v(0)
-        load_v(1)
 
         w1_bf, w1_codes, w1_plane = {}, {}, {}
 
@@ -132,7 +123,7 @@ def tile_list_workshop_offer_score_kernel(
         w2_codes, w2_plane = {}, {}
 
         def deal(b, raw, dtype, name):
-            dealt = held([P, NPASS, PASS], dtype, "%s_%d" % (name, b))
+            dealt = held([P, NPASS, PASS], dtype, name)
             nc.vector.tensor_copy(
                 out=dealt[:].rearrange("p a (t m) -> p a t m", t=PACK),
                 in_=raw[:, :, b * PASS : (b + 1) * PASS].rearrange("p a (m t) -> p a t m", t=PACK),
@@ -140,18 +131,22 @@ def tile_list_workshop_offer_score_kernel(
             return dealt
 
         def deal_w2_codes(b):
-            w2_codes[b] = deal(b, packed["w2"], U16, "w2_codes")
+            w2_codes[b] = deal(b, packed["w2"], U16, "w2_codes_%d" % b)
 
         def deal_w2_plane(b):
-            w2_plane[b] = deal(b, packed["w2_scales"], U8, "w2_plane")
+            w2_plane[b] = deal(b, w2_sc, U8, ("v_sc", "w1_bf_0_0")[b])
 
         def gather(dst, window, offsets):
             nc.vector.tensor_copy(dst, window.indirect(offsets))
 
         g_words = [held([P, S], U32, "g_words_%d" % a) for a in range(NPASS)]
         g_plane = [held([P, S], U8, "g_plane_%d" % a) for a in range(NPASS)]
-        g2_words = [held([P, S2], U32, "g2_words_%d" % b) for b in range(NPASS)]
-        g3_words = [held([P, S2], U32, "g3_words_%d" % b) for b in range(NPASS)]
+        g2_words, g3_words = {}, {}
+
+        def gather_words(picked, b, table, offsets, slot):
+            picked[b] = held([P, S2], U32, slot)
+            gather(picked[b][:], packed[table][:, b, :], offsets[:])
+
         picked_plane = {}
 
         def gather_plane(name, window, offsets, slot):
@@ -215,7 +210,7 @@ def tile_list_workshop_offer_score_kernel(
             reduced[i] = y
 
         def sine(i):
-            s = work.tile([P, 2, HALF], F32, name="wave")
+            s = held([P, 2, HALF], F32, "wave_%d" % i)
             nc.scalar.activation(s[:].rearrange("p u j -> p (u j)"), reduced[i][:], ACT.Sin)
             wave[i] = s
 
@@ -284,45 +279,57 @@ def tile_list_workshop_offer_score_kernel(
                     out_view[:, 2 * mp : 2 * mp + 2, jh * HALF : (jh + 1) * HALF], res[:]
                 )
 
-        for a in range(NPASS):
-            gather(g_plane[a][:], v_sc[:, a, :], idx[:])
+        load_w1(0, 0)
+        load_w1(0, 1)
+        load_v(0)
+        load_v(1)
+        gather(g_plane[0][:], v_sc[:, 0, :], idx[:])
+        gather(g_plane[1][:], v_sc[:, 1, :], idx[:])
         cast_w1(0, 0)
-        cast_w1(0, 1)
-        load_w2_scales()
         load_both_passes("w2", w2_words, H, U16)
-        quantize_w1(0, 0)
-        gather(g_words[0][:], v_words[0][:], idx[:])
+        cast_w1(0, 1)
         load_w1(1, 0)
-        quantize_w1(0, 1)
-        for jh in range(2):
-            gather(g_words[1][:, jh * HALF : (jh + 1) * HALF], v_words[1][:],
-                   idx[:, jh * (HALF // 16) : (jh + 1) * (HALF // 16)])
-        load_w1(1, 1)
-        deal_w2_codes(0)
+        quantize_w1(0, 0)
         deal_w2_plane(0)
-        deal_w2_plane(1)
+        gather(g_words[0][:], v_words[0][:], idx[:])
+        load_w1(1, 1)
+        quantize_w1(0, 1)
+        gather(g_words[1][:, 0:HALF], v_words[1][:], idx[:, 0 : HALF // 16])
+        gather(g_words[1][:, HALF:S], v_words[1][:], idx[:, HALF // 16 : S // 16])
         load_both_passes("v3", tab3_words.rearrange("a p n i -> a p (n i)"), T3, U32)
+        deal_w2_codes(0)
+        cast_w1(1, 0)
+        load_packed_scales("v3_sc", tab3_scales, staged([P, T3], U8))
+        deal_w2_plane(1)
         deal_w2_codes(1)
+        quantize_w1(1, 0)
+        cast_w1(1, 1)
         load_both_passes("v2", tab2_words.rearrange("a p n i -> a p (n i)"), T3, U32)
+        quantize_w1(1, 1)
+        load_packed_scales("v2_sc", tab2_scales, staged([P, T3], U8))
 
         fill = {
-            0: [lambda: cast_w1(1, 0)],
-            1: [lambda: quantize_w1(1, 0), lambda: cast_w1(1, 1)],
-            2: [lambda: quantize_w1(1, 1), lambda: gather_plane("e3", v3_sc, idx3, "plane_0_1")],
-            3: [lambda: weave_h(0, 0, False)],
-            4: [lambda: gather(g3_words[0][:], packed["v3"][:, 0, :], idx3[:]), lambda: quantize_h(0, 0)],
-            5: [lambda: gather(g2_words[0][:], packed["v2"][:, 0, :], idx2[:]), lambda: weave_h(0, 1, False)],
-            6: [lambda: gather_plane("e2", v2_sc, idx2, "plane_1_1"), lambda: gather(g3_words[1][:], packed["v3"][:, 1, :], idx3[:]), lambda: quantize_h(0, 1)],
-            7: [lambda: gather(g2_words[1][:], packed["v2"][:, 1, :], idx2[:]), lambda: weave_h(1, 0, False)],
+            0: [],
+            1: [lambda: gather_words(g3_words, 0, "v3", idx3, "wave_0")],
+            2: [lambda: weave_h(0, 0, False),
+                lambda: gather_plane("e3", packed["v3_sc"], idx3, "wave_1")],
+            3: [lambda: quantize_h(0, 0),
+                lambda: gather_words(g3_words, 1, "v3", idx3, "wave_2")],
+            4: [lambda: weave_h(0, 1, False),
+                lambda: gather_words(g2_words, 0, "v2", idx2, "wave_3")],
+            5: [lambda: quantize_h(0, 1),
+                lambda: gather_plane("e2", packed["v2_sc"], idx2, "wave_4")],
+            6: [lambda: weave_h(1, 0, False),
+                lambda: gather_words(g2_words, 1, "v2", idx2, "wave_5")],
+            7: [lambda: quantize_h(1, 0)],
         }
         n = len(steps)
         for i in range(4):
             products(i)
         count_turns(0)
+        count_turns(1)
         for i in range(n):
             reduce_angle(i)
-            if i + 1 < n:
-                count_turns(i + 1)
             sine(i)
             if i >= 1:
                 combine(i - 1)
@@ -330,8 +337,9 @@ def tile_list_workshop_offer_score_kernel(
                 job()
             if i >= 2 and i + 2 < n:
                 products(i + 2)
+            if i + 2 < n:
+                count_turns(i + 2)
         combine(n - 1)
-        quantize_h(1, 0)
         score_pass(0, 0)
         score_pass(0, 1)
         weave_h(1, 1, True)

@@ -24,7 +24,7 @@ NPASS = 2
 HALF = S // 2
 TWO_PI = 2.0 * math.pi
 TURN_OFFSET = 1024.0
-TURNS_ON_VECTOR = (0, 1,)
+TURNS_ON_VECTOR = (0, 7,)
 
 
 def tile_list_workshop_offer_score_kernel(
@@ -46,9 +46,7 @@ def tile_list_workshop_offer_score_kernel(
         idx3 = keep.tile([P, S2 // 16], U16, name="idx3")
 
         v_sc = held([P, NPASS, T], U8, "v_sc")
-        w2_sc = held([P, NPASS, H], U8, "w2_sc")
         nc.vector.memset(v_sc[:].bitcast(I32), 0)
-        nc.gpsimd.memset(w2_sc[:].bitcast(I32), 0)
 
         def load_scale_rows(queue, plane, dram):
             for q in range(4):
@@ -57,16 +55,20 @@ def tile_list_workshop_offer_score_kernel(
                     dram.bitcast(I32)[:, 4 * q : 4 * q + 4, :].rearrange("a r t -> r a t"),
                 )
 
-        gain_sb = held([P, NPASS, PACK], F32, "gain_sb")
-        least_sb = held([P, S2 // P], F32, "least_sb")
         nc.sync.dma_start(idx[:], offs)
         nc.sync.dma_start(idx3[:], offs3)
         nc.sync.dma_start(idx2[:], offs2)
-        load_scale_rows(nc.scalar, v_sc, tab_scales)
-        load_scale_rows(nc.gpsimd, w2_sc, w2_scales)
-        nc.gpsimd.dma_start(gain_sb[:], gain.rearrange("(b p t) -> p b t", b=NPASS, t=PACK))
-        with nc.allow_non_contiguous_dma(reason="one value of least for each partition"):
-            nc.gpsimd.dma_start(least_sb[:], least.rearrange("(mt p) -> p mt", p=P))
+
+        def load_gain():
+            tile = held([P, NPASS, PACK], F32, "gain_sb")
+            nc.sync.dma_start(tile[:], gain.rearrange("(b p t) -> p b t", b=NPASS, t=PACK))
+            packed["gain"] = tile
+
+        def load_least():
+            tile = held([P, S2 // P], F32, "least_sb")
+            with nc.allow_non_contiguous_dma(reason="one value of least for each partition"):
+                nc.sync.dma_start(tile[:], least.rearrange("(mt p) -> p mt", p=P))
+            packed["least"] = tile
 
         def staged(shape, dtype):
             return stage.tile(shape, dtype, name="staged", align_bytes=64)
@@ -98,16 +100,23 @@ def tile_list_workshop_offer_score_kernel(
                 )
             packed[name] = plane
 
+        def load_w2_scales():
+            plane = held([P, NPASS, H], U8, "w2_sc")
+            nc.vector.memset(plane[:].bitcast(I32), 0)
+            load_scale_rows(nc.sync, plane, w2_scales)
+            packed["w2_sc"] = plane
+
         w1_raw, v_words, packed = {}, {}, {}
 
         w1_bf, w1_codes, w1_plane = {}, {}, {}
 
         def cast_w1(b, a):
             grouped = held([P, PACK, P, PACK], BF16, "w1_bf_%d_%d" % (b, a))
-            nc.scalar.copy(
-                out=grouped[:].rearrange("p t m i -> p m i t"),
-                in_=w1_raw[b, a][:].rearrange("p i (m t) -> p m i t", t=PACK),
-            )
+            for tp in range(2):
+                nc.scalar.copy(
+                    out=grouped[:, 2 * tp : 2 * tp + 2].rearrange("p t m i -> p m i t"),
+                    in_=w1_raw[b, a][:].rearrange("p i (m t) -> p m i t", t=PACK)[:, :, :, 2 * tp : 2 * tp + 2],
+                )
             w1_bf[b, a] = grouped
 
         def quantize_w1(b, a):
@@ -134,7 +143,7 @@ def tile_list_workshop_offer_score_kernel(
             w2_codes[b] = deal(b, packed["w2"], U16, "w2_codes_%d" % b)
 
         def deal_w2_plane(b):
-            w2_plane[b] = deal(b, w2_sc, U8, ("v_sc", "w1_bf_0_0")[b])
+            w2_plane[b] = deal(b, packed["w2_sc"], U8, "w2_plane_%d" % b)
 
         def gather(dst, window, offsets):
             nc.vector.tensor_copy(dst, window.indirect(offsets))
@@ -221,7 +230,7 @@ def tile_list_workshop_offer_score_kernel(
             for u in range(2):
                 t = 2 * tp + u
                 nc.vector.scalar_tensor_tensor(
-                    h_rows[b, jh][:, t, :], wave[i][:, u, :], gain_sb[:, b, t : t + 1],
+                    h_rows[b, jh][:, t, :], wave[i][:, u, :], packed["gain"][:, b, t : t + 1],
                     plain_ps[i][:, u, :], ALU.mult, ALU.add,
                 )
 
@@ -272,56 +281,59 @@ def tile_list_workshop_offer_score_kernel(
                 for u in range(2):
                     mt = 2 * mp + u
                     nc.vector.scalar_tensor_tensor(
-                        res[:, u, :], score_ps[jh, mp, "e2"][:, u, :], least_sb[:, mt : mt + 1],
+                        res[:, u, :], score_ps[jh, mp, "e2"][:, u, :], packed["least"][:, mt : mt + 1],
                         limit[:, u, :], ALU.max, ALU.min,
                     )
                 nc.sync.dma_start(
                     out_view[:, 2 * mp : 2 * mp + 2, jh * HALF : (jh + 1) * HALF], res[:]
                 )
 
+        load_gain()
         load_w1(0, 0)
+        load_scale_rows(nc.sync, v_sc, tab_scales)
         load_w1(0, 1)
+        load_w2_scales()
         load_v(0)
         load_v(1)
+        load_least()
         gather(g_plane[0][:], v_sc[:, 0, :], idx[:])
         gather(g_plane[1][:], v_sc[:, 1, :], idx[:])
         cast_w1(0, 0)
         load_both_passes("w2", w2_words, H, U16)
         cast_w1(0, 1)
         load_w1(1, 0)
-        quantize_w1(0, 0)
         deal_w2_plane(0)
+        quantize_w1(0, 0)
+        deal_w2_plane(1)
         gather(g_words[0][:], v_words[0][:], idx[:])
-        load_w1(1, 1)
+        load_both_passes("v3", tab3_words.rearrange("a p n i -> a p (n i)"), T3, U32)
         quantize_w1(0, 1)
         gather(g_words[1][:, 0:HALF], v_words[1][:], idx[:, 0 : HALF // 16])
         gather(g_words[1][:, HALF:S], v_words[1][:], idx[:, HALF // 16 : S // 16])
-        load_both_passes("v3", tab3_words.rearrange("a p n i -> a p (n i)"), T3, U32)
+        load_w1(1, 1)
         deal_w2_codes(0)
-        cast_w1(1, 0)
-        load_packed_scales("v3_sc", tab3_scales, staged([P, T3], U8))
-        deal_w2_plane(1)
-        deal_w2_codes(1)
-        quantize_w1(1, 0)
-        cast_w1(1, 1)
-        load_both_passes("v2", tab2_words.rearrange("a p n i -> a p (n i)"), T3, U32)
-        quantize_w1(1, 1)
-        load_packed_scales("v2_sc", tab2_scales, staged([P, T3], U8))
 
         fill = {
-            0: [],
-            1: [lambda: gather_words(g3_words, 0, "v3", idx3, "wave_0")],
-            2: [lambda: weave_h(0, 0, False),
-                lambda: gather_plane("e3", packed["v3_sc"], idx3, "wave_1")],
-            3: [lambda: quantize_h(0, 0),
-                lambda: gather_words(g3_words, 1, "v3", idx3, "wave_2")],
-            4: [lambda: weave_h(0, 1, False),
-                lambda: gather_words(g2_words, 0, "v2", idx2, "wave_3")],
-            5: [lambda: quantize_h(0, 1),
-                lambda: gather_plane("e2", packed["v2_sc"], idx2, "wave_4")],
+            0: [lambda: deal_w2_codes(1),
+                lambda: load_both_passes("v2", tab2_words.rearrange("a p n i -> a p (n i)"), T3, U32),
+                lambda: cast_w1(1, 0),
+                lambda: load_packed_scales("v3_sc", tab3_scales, staged([P, T3], U8))],
+            1: [lambda: cast_w1(1, 1),
+                lambda: quantize_w1(1, 0),
+                lambda: load_packed_scales("v2_sc", tab2_scales, staged([P, T3], U8)),
+                lambda: quantize_w1(1, 1)],
+            2: [lambda: weave_h(0, 0, False)],
+            3: [lambda: quantize_h(0, 0)],
+            4: [lambda: weave_h(0, 1, False)],
+            5: [lambda: quantize_h(0, 1)],
             6: [lambda: weave_h(1, 0, False),
-                lambda: gather_words(g2_words, 1, "v2", idx2, "wave_5")],
-            7: [lambda: quantize_h(1, 0)],
+                lambda: quantize_h(1, 0)],
+            7: [lambda: gather_words(g3_words, 0, "v3", idx3, "own_g30"),
+                lambda: gather_words(g3_words, 1, "v3", idx3, "own_g31"),
+                lambda: gather_words(g2_words, 0, "v2", idx2, "own_g20"),
+                lambda: gather_plane("e3", packed["v3_sc"], idx3, "own_p3"),
+                lambda: gather_words(g2_words, 1, "v2", idx2, "own_g21"),
+                lambda: gather_plane("e2", packed["v2_sc"], idx2, "own_p2")],
         }
         n = len(steps)
         for i in range(4):

@@ -21,10 +21,35 @@ P = 128
 PACK = 4
 PASS = P * PACK
 NPASS = 2
+QUADRANTS = 4
 HALF = S // 2
+LIST_HALF = HALF // 16
+BANKS = 8
 TWO_PI = 2.0 * math.pi
+
+STEPS = [(b, jh, tp) for b in range(NPASS) for jh in range(2) for tp in range(2)]
+STEPS_IN_PSUM = BANKS // 2
+LOOKAHEAD = 2
+
 TURN_OFFSET = 1024.0
-TURNS_ON_VECTOR = (0, 7,)
+TURNS_ON_VECTOR = (0, len(STEPS) - 1)
+
+KIB = 1024
+PLACE = {
+    "v_sc": 0, "g_words_0": 0, "w1_codes_0_0": 2 * KIB,
+    "w1_bf_0_0": 4 * KIB, "gain": 4 * KIB, "w1_codes_0_1": 4 * KIB + 64,
+    "w1_bf_0_1": 8 * KIB, "g_words_1": 8 * KIB,
+    "w1_raw_0_0": 12 * KIB, "w2": 12 * KIB, "v2_0": 12 * KIB,
+    "w1_raw_0_1": 20 * KIB, "w2_sc": 20 * KIB, "v2_1": 20 * KIB,
+    "w1_raw_1_0": 24 * KIB, "v3_sc": 24 * KIB, "wave_0": 25 * KIB,
+    "v_words_0": 32 * KIB, "w1_plane_0_1": 32 * KIB,
+    "w1_raw_1_1": 32 * KIB + 512, "v2_sc": 32 * KIB + 512, "wave_2": 33 * KIB + 512,
+    "v_words_1": 40 * KIB + 512, "w2_plane_0": 40 * KIB + 512, "w2_codes_0": 41 * KIB + 512,
+    "v3_0": 43 * KIB + 512, "v3_1": 47 * KIB + 512,
+    "turns_1": 51 * KIB + 512, "w1_bf_1_0": 51 * KIB + 512, "least": 51 * KIB + 512,
+    "reduced_0": 55 * KIB + 512, "w1_bf_1_1": 55 * KIB + 512,
+    "back_1": 59 * KIB + 512, "w2_plane_1": 59 * KIB + 512, "w2_codes_1": 60 * KIB + 512,
+}
 
 
 def tile_list_workshop_offer_score_kernel(
@@ -34,94 +59,102 @@ def tile_list_workshop_offer_score_kernel(
     nc = tc.nc
     with ExitStack() as ctx:
         keep = ctx.enter_context(tc.tile_pool(name="keep", bufs=1))
-        work = ctx.enter_context(tc.tile_pool(name="work", bufs=4))
-        stage = ctx.enter_context(tc.tile_pool(name="stage", bufs=4))
-        psum = ctx.enter_context(tc.psum_pool(name="psum", bufs=8))
+        limits = ctx.enter_context(tc.tile_pool(name="limits", bufs=S2 // P))
+        reused = ctx.enter_context(tc.tile_pool(name="reused", bufs=1))
+        psum = ctx.enter_context(tc.psum_pool(name="psum", bufs=BANKS))
 
-        def held(shape, dtype, name):
+        def sbuf(shape, dtype, name):
+            if name in PLACE:
+                return reused.tile(shape, dtype, name=name, align_bytes=64, offset=PLACE[name])
             return keep.tile(shape, dtype, name=name, align_bytes=64)
 
         idx = keep.tile([P, S // 16], U16, name="idx")
         idx2 = keep.tile([P, S2 // 16], U16, name="idx2")
         idx3 = keep.tile([P, S2 // 16], U16, name="idx3")
+        lists = {"v2": idx2, "v3": idx3}
+        table_words = {"v2": tab2_words, "v3": tab3_words}
+        table_scales = {"v2": tab2_scales, "v3": tab3_scales}
 
-        v_sc = held([P, NPASS, T], U8, "v_sc")
+        v_sc = sbuf([P, NPASS, T], U8, "v_sc")
         nc.vector.memset(v_sc[:].bitcast(I32), 0)
-
-        def load_scale_rows(queue, plane, dram):
-            for q in range(4):
-                queue.dma_start(
-                    plane[32 * q : 32 * q + 4, :, :].bitcast(I32),
-                    dram.bitcast(I32)[:, 4 * q : 4 * q + 4, :].rearrange("a r t -> r a t"),
-                )
-
         nc.sync.dma_start(idx[:], offs)
         nc.sync.dma_start(idx3[:], offs3)
         nc.sync.dma_start(idx2[:], offs2)
 
-        def load_gain():
-            tile = held([P, NPASS, PACK], F32, "gain_sb")
-            nc.sync.dma_start(tile[:], gain.rearrange("(b p t) -> p b t", b=NPASS, t=PACK))
-            packed["gain"] = tile
+        loaded = {}
 
-        def load_least():
-            tile = held([P, S2 // P], F32, "least_sb")
-            with nc.allow_non_contiguous_dma(reason="one value of least for each partition"):
-                nc.sync.dma_start(tile[:], least.rearrange("(mt p) -> p mt", p=P))
-            packed["least"] = tile
-
-        def staged(shape, dtype):
-            return stage.tile(shape, dtype, name="staged", align_bytes=64)
-
-        def load_w1(b, a):
-            raw = staged([P, PACK, PASS], F32)
-            rows = w1[a * PASS : (a + 1) * PASS, b * PASS : (b + 1) * PASS]
-            nc.sync.dma_start(raw[:], rows.rearrange("(p i) c -> p i c", i=PACK))
-            w1_raw[b, a] = raw
-
-        def load_v(a):
-            words = staged([P, T], U32)
-            nc.sync.dma_start(
-                words[:].bitcast(I32), tab_words[a].rearrange("p n i -> p (n i)").bitcast(I32)
-            )
-            v_words[a] = words
-
-        def load_both_passes(name, dram, width, dtype):
-            words = staged([P, NPASS, width], dtype)
-            nc.sync.dma_start(words[:].bitcast(I32), dram.bitcast(I32).rearrange("a p c -> p a c"))
-            packed[name] = words
-
-        def load_packed_scales(name, dram, plane):
-            nc.gpsimd.memset(plane[:].bitcast(I32), 0)
-            for q in range(4):
-                nc.sync.dma_start(
-                    plane[32 * q : 32 * q + 8, :].bitcast(I32),
-                    dram.bitcast(I32)[:, 4 * q : 4 * q + 4, :],
+        def load_planes_side_by_side(planes, dram):
+            for q in range(QUADRANTS):
+                nc.scalar.dma_start(
+                    planes[32 * q : 32 * q + 4, :, :].bitcast(I32),
+                    dram.bitcast(I32)[:, 4 * q : 4 * q + 4, :].rearrange("a s t -> s a t"),
                 )
-            packed[name] = plane
 
         def load_w2_scales():
-            plane = held([P, NPASS, H], U8, "w2_sc")
-            nc.vector.memset(plane[:].bitcast(I32), 0)
-            load_scale_rows(nc.sync, plane, w2_scales)
-            packed["w2_sc"] = plane
+            planes = sbuf([P, NPASS, H], U8, "w2_sc")
+            nc.gpsimd.memset(planes[:].bitcast(I32), 0)
+            load_planes_side_by_side(planes, w2_scales)
+            loaded["w2_sc"] = planes
 
-        w1_raw, v_words, packed = {}, {}, {}
+        def load_table_scales(table):
+            planes = sbuf([P, T3], U8, table + "_sc")
+            nc.gpsimd.memset(planes[:].bitcast(I32), 0)
+            for q in range(QUADRANTS):
+                nc.sync.dma_start(
+                    planes[32 * q : 32 * q + 8, :].bitcast(I32),
+                    table_scales[table].bitcast(I32)[:, 4 * q : 4 * q + 4, :],
+                )
+            loaded[table + "_sc"] = planes
 
-        w1_bf, w1_codes, w1_plane = {}, {}, {}
+        def load_words(name, dram, a, width):
+            words = sbuf([P, width], U32, name)
+            nc.sync.dma_start(
+                words[:].bitcast(I32), dram[a].rearrange("p n i -> p (n i)").bitcast(I32)
+            )
+            loaded[name] = words
+
+        def load_table_words(table, b):
+            load_words("%s_%d" % (table, b), table_words[table], b, T3)
+
+        def load_w1(b, a):
+            raw = sbuf([P, PACK, PASS], F32, "w1_raw_%d_%d" % (b, a))
+            rows = w1[a * PASS : (a + 1) * PASS, b * PASS : (b + 1) * PASS]
+            nc.sync.dma_start(raw[:], rows.rearrange("(p i) c -> p i c", i=PACK))
+            loaded["w1", b, a] = raw
+
+        def load_w2():
+            words = sbuf([P, NPASS, H], U16, "w2")
+            nc.sync.dma_start(
+                words[:].bitcast(I32), w2_words.bitcast(I32).rearrange("a p c -> p a c")
+            )
+            loaded["w2"] = words
+
+        def load_gain():
+            tile = sbuf([P, NPASS, PACK], F32, "gain")
+            nc.sync.dma_start(tile[:], gain.rearrange("(b p t) -> p b t", b=NPASS, t=PACK))
+            loaded["gain"] = tile
+
+        def load_least():
+            tile = sbuf([P, S2 // P], F32, "least")
+            with nc.allow_non_contiguous_dma(reason="one value of least for each partition"):
+                nc.sync.dma_start(tile[:], least.rearrange("(mt p) -> p mt", p=P))
+            loaded["least"] = tile
+
+        w1_bf, w1_codes, w1_plane, w2_codes, w2_plane = {}, {}, {}, {}, {}
 
         def cast_w1(b, a):
-            grouped = held([P, PACK, P, PACK], BF16, "w1_bf_%d_%d" % (b, a))
+            grouped = sbuf([P, PACK, P, PACK], BF16, "w1_bf_%d_%d" % (b, a))
+            source = loaded["w1", b, a][:].rearrange("p i (m t) -> p m i t", t=PACK)
             for tp in range(2):
                 nc.scalar.copy(
                     out=grouped[:, 2 * tp : 2 * tp + 2].rearrange("p t m i -> p m i t"),
-                    in_=w1_raw[b, a][:].rearrange("p i (m t) -> p m i t", t=PACK)[:, :, :, 2 * tp : 2 * tp + 2],
+                    in_=source[:, :, :, 2 * tp : 2 * tp + 2],
                 )
             w1_bf[b, a] = grouped
 
         def quantize_w1(b, a):
-            codes = held([P, PASS], U32, "w1_codes_%d_%d" % (b, a))
-            plane = held([P, PASS], U8, "plane_%d_%d" % (b, a))
+            codes = sbuf([P, PASS], U32, "w1_codes_%d_%d" % (b, a))
+            plane = sbuf([P, PASS], U8, "w1_plane_%d_%d" % (b, a))
             nc.vector.quantize_mx(
                 out=codes[:].bitcast(E4M3),
                 scales=plane[:],
@@ -129,89 +162,88 @@ def tile_list_workshop_offer_score_kernel(
             )
             w1_codes[b, a], w1_plane[b, a] = codes, plane
 
-        w2_codes, w2_plane = {}, {}
-
-        def deal(b, raw, dtype, name):
-            dealt = held([P, NPASS, PASS], dtype, name)
+        def reorder_columns(b, raw, dtype, name):
+            ordered = sbuf([P, NPASS, PASS], dtype, name)
             nc.vector.tensor_copy(
-                out=dealt[:].rearrange("p a (t m) -> p a t m", t=PACK),
+                out=ordered[:].rearrange("p a (t m) -> p a t m", t=PACK),
                 in_=raw[:, :, b * PASS : (b + 1) * PASS].rearrange("p a (m t) -> p a t m", t=PACK),
             )
-            return dealt
+            return ordered
 
-        def deal_w2_codes(b):
-            w2_codes[b] = deal(b, packed["w2"], U16, "w2_codes_%d" % b)
+        def reorder_w2_codes(b):
+            w2_codes[b] = reorder_columns(b, loaded["w2"], U16, "w2_codes_%d" % b)
 
-        def deal_w2_plane(b):
-            w2_plane[b] = deal(b, packed["w2_sc"], U8, "w2_plane_%d" % b)
+        def reorder_w2_plane(b):
+            w2_plane[b] = reorder_columns(b, loaded["w2_sc"], U8, "w2_plane_%d" % b)
+
+        g_words = {}
+        g_plane = [sbuf([P, S], U8, "g_plane_%d" % a) for a in range(NPASS)]
+        picked_words, picked_planes = {}, {}
 
         def gather(dst, window, offsets):
             nc.vector.tensor_copy(dst, window.indirect(offsets))
 
-        g_words = [held([P, S], U32, "g_words_%d" % a) for a in range(NPASS)]
-        g_plane = [held([P, S], U8, "g_plane_%d" % a) for a in range(NPASS)]
-        g2_words, g3_words = {}, {}
+        def gather_table_words(table, b):
+            picked = sbuf([P, S2], U32, "picked_%s_%d" % (table, b))
+            gather(picked[:], loaded["%s_%d" % (table, b)][:], lists[table][:])
+            picked_words[table, b] = picked
 
-        def gather_words(picked, b, table, offsets, slot):
-            picked[b] = held([P, S2], U32, slot)
-            gather(picked[b][:], packed[table][:, b, :], offsets[:])
+        def gather_table_planes(table):
+            picked = sbuf([P, S2], U8, "picked_%s_sc" % table)
+            gather(picked[:], loaded[table + "_sc"][:], lists[table][:])
+            picked_planes[table] = picked
 
-        picked_plane = {}
+        angle_ps, plain_ps, turns, reduced, wave = {}, {}, {}, {}, {}
+        h_rows, h_bf, h_codes, h_plane = {}, {}, {}, {}
 
-        def gather_plane(name, window, offsets, slot):
-            plane = held([P, S2], U8, slot)
-            gather(plane[:], window[:], offsets[:])
-            picked_plane[name] = plane
-
-        steps = [(b, jh, tp) for b in range(NPASS) for jh in range(2) for tp in range(2)]
-        angle_ps, plain_ps, reduced, wave, h_rows = {}, {}, {}, {}, {}
-        h_bf, h_codes, h_plane = {}, {}, {}
-
-        def products(i):
-            b, jh, tp = steps[i]
+        def angle_product(i):
+            b, jh, tp = STEPS[i]
             cols = slice(jh * HALF, (jh + 1) * HALF)
-            x = psum.tile([P, 2, HALF], F32, name="bank")
+            bank = psum.tile([P, 2, HALF], F32, name="bank")
             for a in range(NPASS):
                 for u in range(2):
                     m = slice((2 * tp + u) * P, (2 * tp + u + 1) * P)
                     nc.tensor.matmul_mx(
-                        out=x[:, u, :],
+                        out=bank[:, u, :],
                         lhsT=w1_codes[b, a][:, m].bitcast(E4M3), lhsT_scale=w1_plane[b, a][:, m],
                         rhs=g_words[a][:, cols].bitcast(E4M3), rhs_scale=g_plane[a][:, cols],
                         start=(a == 0 and u == 0), stop=(a == NPASS - 1 and u == 1),
                     )
-            y = psum.tile([P, 2, HALF], F32, name="bank")
+            angle_ps[i] = bank
+
+        def plain_product(i):
+            b, jh, tp = STEPS[i]
+            cols = slice(jh * HALF, (jh + 1) * HALF)
+            bank = psum.tile([P, 2, HALF], F32, name="bank")
             for u in range(2):
                 m = slice((2 * tp + u) * P, (2 * tp + u + 1) * P)
                 for a in range(NPASS):
                     nc.tensor.matmul_mx(
-                        out=y[:, u, :],
+                        out=bank[:, u, :],
                         lhsT=w2_codes[b][:, a, m].bitcast(E2M1), lhsT_scale=w2_plane[b][:, a, m],
                         rhs=g_words[a][:, cols].bitcast(E4M3), rhs_scale=g_plane[a][:, cols],
                         start=(a == 0), stop=(a == NPASS - 1),
                     )
-            angle_ps[i], plain_ps[i] = x, y
-
-        turns = {}
+            plain_ps[i] = bank
 
         def count_turns(i):
             x = angle_ps[i][:].rearrange("p u j -> p (u j)")
             if i in TURNS_ON_VECTOR:
-                k = work.tile([P, 2 * HALF], I32, name="turns_i")
-                nc.vector.tensor_scalar(k[:], x, 1.0 / TWO_PI, None, ALU.mult)
-                turns[i] = k
+                n = sbuf([P, 2 * HALF], I32, "turns_%d" % i)
+                nc.vector.tensor_scalar(n[:], x, 1.0 / TWO_PI, None, ALU.mult)
+                turns[i] = n
             else:
-                k = work.tile([P, 2 * HALF], U32, name="turns_u")
-                nc.scalar.activation(k[:], x, ACT.Copy, bias=TURN_OFFSET, scale=1.0 / TWO_PI)
-                back = work.tile([P, 2 * HALF], F32, name="back")
+                n = sbuf([P, 2 * HALF], U32, "turns_%d" % i)
+                nc.scalar.activation(n[:], x, ACT.Copy, bias=TURN_OFFSET, scale=1.0 / TWO_PI)
+                back = sbuf([P, 2 * HALF], F32, "back_%d" % i)
                 nc.scalar.activation(
-                    back[:], k[:], ACT.Copy, bias=TURN_OFFSET * TWO_PI, scale=-TWO_PI
+                    back[:], n[:], ACT.Copy, bias=TURN_OFFSET * TWO_PI, scale=-TWO_PI
                 )
                 turns[i] = back
 
         def reduce_angle(i):
             x = angle_ps[i][:].rearrange("p u j -> p (u j)")
-            y = work.tile([P, 2 * HALF], F32, name="reduced")
+            y = sbuf([P, 2 * HALF], F32, "reduced_%d" % i)
             if i in TURNS_ON_VECTOR:
                 nc.vector.scalar_tensor_tensor(y[:], turns[i][:], -TWO_PI, x, ALU.mult, ALU.add)
             else:
@@ -219,34 +251,32 @@ def tile_list_workshop_offer_score_kernel(
             reduced[i] = y
 
         def sine(i):
-            s = held([P, 2, HALF], F32, "wave_%d" % i)
+            s = sbuf([P, 2, HALF], F32, "wave_%d" % i)
             nc.scalar.activation(s[:].rearrange("p u j -> p (u j)"), reduced[i][:], ACT.Sin)
             wave[i] = s
 
         def combine(i):
-            b, jh, tp = steps[i]
+            b, jh, tp = STEPS[i]
             if tp == 0:
-                h_rows[b, jh] = held([P, PACK, HALF], BF16, "h_rows_%d_%d" % (b, jh))
+                h_rows[b, jh] = sbuf([P, PACK, HALF], BF16, "h_rows_%d_%d" % (b, jh))
             for u in range(2):
                 t = 2 * tp + u
                 nc.vector.scalar_tensor_tensor(
-                    h_rows[b, jh][:, t, :], wave[i][:, u, :], packed["gain"][:, b, t : t + 1],
+                    h_rows[b, jh][:, t, :], wave[i][:, u, :], loaded["gain"][:, b, t : t + 1],
                     plain_ps[i][:, u, :], ALU.mult, ALU.add,
                 )
 
-        def weave_h(b, jh, on_vector):
-            grouped = held([P, HALF, PACK], BF16, "h_bf_%d_%d" % (b, jh))
-            dst = grouped[:].rearrange("p (c i) t -> p c t i", i=4)
-            src = h_rows[b, jh][:].rearrange("p t (c i) -> p c t i", i=4)
-            if on_vector:
-                nc.vector.tensor_copy(out=dst, in_=src)
-            else:
-                nc.scalar.copy(out=dst, in_=src)
+        def interleave_h(b, jh, copy):
+            grouped = sbuf([P, HALF, PACK], BF16, "h_bf_%d_%d" % (b, jh))
+            copy(
+                out=grouped[:].rearrange("p (c i) t -> p c t i", i=4),
+                in_=h_rows[b, jh][:].rearrange("p t (c i) -> p c t i", i=4),
+            )
             h_bf[b, jh] = grouped
 
         def quantize_h(b, jh):
-            codes = held([P, HALF], U32, "h_codes_%d_%d" % (b, jh))
-            plane = held([P, HALF], U8, "h_plane_%d_%d" % (b, jh))
+            codes = sbuf([P, HALF], U32, "h_codes_%d_%d" % (b, jh))
+            plane = sbuf([P, HALF], U8, "h_plane_%d_%d" % (b, jh))
             nc.vector.quantize_mx(
                 out=codes[:].bitcast(E4M3), scales=plane[:],
                 in_=h_bf[b, jh][:].rearrange("p j t -> p (j t)"),
@@ -257,16 +287,16 @@ def tile_list_workshop_offer_score_kernel(
 
         def score_pass(jh, b):
             for mp in range(2):
-                for name, words in (("e3", g3_words), ("e2", g2_words)):
-                    plane = picked_plane[name]
+                for table in ("v3", "v2"):
                     if b == 0:
-                        score_ps[jh, mp, name] = psum.tile([P, 2, HALF], F32, name="bank")
-                    bank = score_ps[jh, mp, name]
+                        score_ps[jh, mp, table] = psum.tile([P, 2, HALF], F32, name="bank")
+                    bank = score_ps[jh, mp, table]
                     for u in range(2):
                         m = slice((2 * mp + u) * P, (2 * mp + u + 1) * P)
                         nc.tensor.matmul_mx(
                             out=bank[:, u, :],
-                            lhsT=words[b][:, m].bitcast(E4M3), lhsT_scale=plane[4 * b : P, m],
+                            lhsT=picked_words[table, b][:, m].bitcast(E4M3),
+                            lhsT_scale=picked_planes[table][4 * b : P, m],
                             rhs=h_codes[b, jh][:].bitcast(E4M3), rhs_scale=h_plane[b, jh][:],
                             start=(b == 0 and u == 0), stop=(b == NPASS - 1 and u == 1),
                         )
@@ -275,86 +305,102 @@ def tile_list_workshop_offer_score_kernel(
 
         def finish(jh):
             for mp in range(2):
-                limit = work.tile([P, 2, HALF], F32, name="limit")
-                nc.scalar.copy(out=limit[:], in_=score_ps[jh, mp, "e3"][:])
-                res = held([P, 2, HALF], F32, "res_%d_%d" % (jh, mp))
+                limit = limits.tile([P, 2, HALF], F32, name="limit")
+                nc.scalar.copy(out=limit[:], in_=score_ps[jh, mp, "v3"][:])
+                res = sbuf([P, 2, HALF], F32, "res_%d_%d" % (jh, mp))
                 for u in range(2):
                     mt = 2 * mp + u
                     nc.vector.scalar_tensor_tensor(
-                        res[:, u, :], score_ps[jh, mp, "e2"][:, u, :], packed["least"][:, mt : mt + 1],
-                        limit[:, u, :], ALU.max, ALU.min,
+                        res[:, u, :], score_ps[jh, mp, "v2"][:, u, :],
+                        loaded["least"][:, mt : mt + 1], limit[:, u, :], ALU.max, ALU.min,
                     )
                 nc.sync.dma_start(
                     out_view[:, 2 * mp : 2 * mp + 2, jh * HALF : (jh + 1) * HALF], res[:]
                 )
 
-        load_gain()
         load_w1(0, 0)
-        load_scale_rows(nc.sync, v_sc, tab_scales)
         load_w1(0, 1)
-        load_w2_scales()
-        load_v(0)
-        load_v(1)
-        load_least()
-        gather(g_plane[0][:], v_sc[:, 0, :], idx[:])
-        gather(g_plane[1][:], v_sc[:, 1, :], idx[:])
+        for a in range(NPASS):
+            load_words("v_words_%d" % a, tab_words, a, T)
+        load_planes_side_by_side(v_sc, tab_scales)
+        warm_in = sbuf([P, 1], F32, "warm_in")
+        nc.vector.memset(warm_in[:], 0.0)
+        warm_out = sbuf([P, 1], F32, "warm_out")
+        nc.scalar.activation(warm_out[:], warm_in[:], ACT.Sin)
+        for a in range(NPASS):
+            gather(g_plane[a][:], v_sc[:, a, :], idx[:])
         cast_w1(0, 0)
-        load_both_passes("w2", w2_words, H, U16)
+        load_w2()
         cast_w1(0, 1)
+        load_w2_scales()
         load_w1(1, 0)
-        deal_w2_plane(0)
         quantize_w1(0, 0)
-        deal_w2_plane(1)
-        gather(g_words[0][:], v_words[0][:], idx[:])
-        load_both_passes("v3", tab3_words.rearrange("a p n i -> a p (n i)"), T3, U32)
-        quantize_w1(0, 1)
-        gather(g_words[1][:, 0:HALF], v_words[1][:], idx[:, 0 : HALF // 16])
-        gather(g_words[1][:, HALF:S], v_words[1][:], idx[:, HALF // 16 : S // 16])
+        load_gain()
+        g_words[0] = sbuf([P, S], U32, "g_words_0")
+        gather(g_words[0][:], loaded["v_words_0"][:], idx[:])
         load_w1(1, 1)
-        deal_w2_codes(0)
+        quantize_w1(0, 1)
+        g_words[1] = sbuf([P, S], U32, "g_words_1")
+        for jh in range(2):
+            gather(
+                g_words[1][:, jh * HALF : (jh + 1) * HALF], loaded["v_words_1"][:],
+                idx[:, jh * LIST_HALF : (jh + 1) * LIST_HALF],
+            )
+        for b in range(NPASS):
+            load_table_words("v3", b)
+        reorder_w2_plane(0)
+        reorder_w2_codes(0)
 
-        fill = {
-            0: [lambda: deal_w2_codes(1),
-                lambda: load_both_passes("v2", tab2_words.rearrange("a p n i -> a p (n i)"), T3, U32),
-                lambda: cast_w1(1, 0),
-                lambda: load_packed_scales("v3_sc", tab3_scales, staged([P, T3], U8))],
-            1: [lambda: cast_w1(1, 1),
-                lambda: quantize_w1(1, 0),
-                lambda: load_packed_scales("v2_sc", tab2_scales, staged([P, T3], U8)),
-                lambda: quantize_w1(1, 1)],
-            2: [lambda: weave_h(0, 0, False)],
-            3: [lambda: quantize_h(0, 0)],
-            4: [lambda: weave_h(0, 1, False)],
-            5: [lambda: quantize_h(0, 1)],
-            6: [lambda: weave_h(1, 0, False),
-                lambda: quantize_h(1, 0)],
-            7: [lambda: gather_words(g3_words, 0, "v3", idx3, "own_g30"),
-                lambda: gather_words(g3_words, 1, "v3", idx3, "own_g31"),
-                lambda: gather_words(g2_words, 0, "v2", idx2, "own_g20"),
-                lambda: gather_plane("e3", packed["v3_sc"], idx3, "own_p3"),
-                lambda: gather_words(g2_words, 1, "v2", idx2, "own_g21"),
-                lambda: gather_plane("e2", packed["v2_sc"], idx2, "own_p2")],
+        def prepare_second_group(a):
+            cast_w1(1, a)
+            load_table_scales(("v3", "v2")[a])
+            quantize_w1(1, a)
+
+        late_gathers = {
+            1: [lambda: gather_table_words("v3", 0)],
+            2: [lambda: gather_table_words("v3", 1)],
+            3: [lambda: gather_table_planes("v3")],
+            4: [lambda: gather_table_words("v2", 0)],
+            5: [lambda: gather_table_words("v2", 1), lambda: gather_table_planes("v2")],
         }
-        n = len(steps)
-        for i in range(4):
-            products(i)
-        count_turns(0)
-        count_turns(1)
-        for i in range(n):
+
+        for i in range(STEPS_IN_PSUM):
+            angle_product(i)
+        for i in range(STEPS_IN_PSUM):
+            plain_product(i)
+        for i in range(LOOKAHEAD):
+            count_turns(i)
+        for i in range(len(STEPS)):
             reduce_angle(i)
             sine(i)
             if i >= 1:
                 combine(i - 1)
-            for job in fill.get(i, []):
+            if i == 0:
+                reorder_w2_codes(1)
+                load_table_words("v2", 0)
+                reorder_w2_plane(1)
+                load_table_words("v2", 1)
+                prepare_second_group(0)
+                load_least()
+            elif i == 1:
+                prepare_second_group(1)
+            elif i % 2 == 0:
+                interleave_h(*STEPS[i - 1][:2], nc.scalar.copy)
+            else:
+                quantize_h(*STEPS[i - 2][:2])
+            for job in late_gathers.get(i, []):
                 job()
-            if i >= 2 and i + 2 < n:
-                products(i + 2)
-            if i + 2 < n:
-                count_turns(i + 2)
-        combine(n - 1)
+            ahead = i + LOOKAHEAD
+            if ahead < len(STEPS):
+                if ahead >= STEPS_IN_PSUM:
+                    angle_product(ahead)
+                    plain_product(ahead)
+                count_turns(ahead)
+        combine(len(STEPS) - 1)
+
         score_pass(0, 0)
         score_pass(0, 1)
-        weave_h(1, 1, True)
+        interleave_h(1, 1, nc.vector.tensor_copy)
         score_pass(1, 0)
         finish(0)
         quantize_h(1, 1)

import math
from contextlib import ExitStack

import concourse.mybir as mybir

K, H, T, S, T3, S2 = 1024, 1024, 2048, 512, 1024, 512
FLOPS = 2 * (2 * K * H * S + 2 * H * S2 * S)

F32 = mybir.dt.float32
BF16 = mybir.dt.bfloat16
I32 = mybir.dt.int32
U32 = mybir.dt.uint32
U16 = mybir.dt.uint16
U8 = mybir.dt.uint8
E4M3 = mybir.dt.float8_e4m3fn_x4
E2M1 = mybir.dt.float4_e2m1fn_x4
ALU = mybir.AluOpType
ACT = mybir.ActivationFunctionType

P = 128
PACK = 4
PASS = P * PACK
NPASS = 2
QUADRANTS = 4
HALF = S // 2
LIST_HALF = HALF // 16
BANKS = 8
TWO_PI = 2.0 * math.pi

STEPS = [(b, jh, tp) for b in range(NPASS) for jh in range(2) for tp in range(2)]
STEPS_IN_PSUM = BANKS // 2
LOOKAHEAD = 2

TURN_OFFSET = 1024.0
TURNS_ON_VECTOR = (0, len(STEPS) - 1)

KIB = 1024
PLACE = {
    "v_sc": 0, "g_words_0": 0, "w1_codes_0_0": 2 * KIB,
    "w1_bf_0_0": 4 * KIB, "gain": 4 * KIB, "w1_codes_0_1": 4 * KIB + 64,
    "w1_bf_0_1": 8 * KIB, "g_words_1": 8 * KIB,
    "w1_raw_0_0": 12 * KIB, "w2": 12 * KIB, "v2_0": 12 * KIB,
    "w1_raw_0_1": 20 * KIB, "w2_sc": 20 * KIB, "v2_1": 20 * KIB,
    "w1_raw_1_0": 24 * KIB, "v3_sc": 24 * KIB, "wave_0": 25 * KIB,
    "v_words_0": 32 * KIB, "w1_plane_0_1": 32 * KIB,
    "w1_raw_1_1": 32 * KIB + 512, "v2_sc": 32 * KIB + 512, "wave_2": 33 * KIB + 512,
    "v_words_1": 40 * KIB + 512, "w2_plane_0": 40 * KIB + 512, "w2_codes_0": 41 * KIB + 512,
    "v3_0": 43 * KIB + 512, "v3_1": 47 * KIB + 512,
    "turns_1": 51 * KIB + 512, "w1_bf_1_0": 51 * KIB + 512, "least": 51 * KIB + 512,
    "reduced_0": 55 * KIB + 512, "w1_bf_1_1": 55 * KIB + 512,
    "back_1": 59 * KIB + 512, "w2_plane_1": 59 * KIB + 512, "w2_codes_1": 60 * KIB + 512,
}


def tile_list_workshop_offer_score_kernel(
    tc, tab_words, tab_scales, tab2_words, tab2_scales, tab3_words, tab3_scales,
    offs, offs2, offs3, w1, w2_words, w2_scales, gain, least, out,
):
    nc = tc.nc
    with ExitStack() as ctx:
        keep = ctx.enter_context(tc.tile_pool(name="keep", bufs=1))
        limits = ctx.enter_context(tc.tile_pool(name="limits", bufs=S2 // P))
        reused = ctx.enter_context(tc.tile_pool(name="reused", bufs=1))
        psum = ctx.enter_context(tc.psum_pool(name="psum", bufs=BANKS))

        def sbuf(shape, dtype, name):
            if name in PLACE:
                return reused.tile(shape, dtype, name=name, align_bytes=64, offset=PLACE[name])
            return keep.tile(shape, dtype, name=name, align_bytes=64)

        idx = keep.tile([P, S // 16], U16, name="idx")
        idx2 = keep.tile([P, S2 // 16], U16, name="idx2")
        idx3 = keep.tile([P, S2 // 16], U16, name="idx3")
        lists = {"v2": idx2, "v3": idx3}
        table_words = {"v2": tab2_words, "v3": tab3_words}
        table_scales = {"v2": tab2_scales, "v3": tab3_scales}

        v_sc = sbuf([P, NPASS, T], U8, "v_sc")
        nc.vector.memset(v_sc[:].bitcast(I32), 0)
        nc.sync.dma_start(idx[:], offs)
        nc.sync.dma_start(idx3[:], offs3)
        nc.sync.dma_start(idx2[:], offs2)

        loaded = {}

        def load_planes_side_by_side(planes, dram):
            for q in range(QUADRANTS):
                nc.scalar.dma_start(
                    planes[32 * q : 32 * q + 4, :, :].bitcast(I32),
                    dram.bitcast(I32)[:, 4 * q : 4 * q + 4, :].rearrange("a s t -> s a t"),
                )

        def load_w2_scales():
            planes = sbuf([P, NPASS, H], U8, "w2_sc")
            nc.gpsimd.memset(planes[:].bitcast(I32), 0)
            load_planes_side_by_side(planes, w2_scales)
            loaded["w2_sc"] = planes

        def load_table_scales(table):
            planes = sbuf([P, T3], U8, table + "_sc")
            nc.gpsimd.memset(planes[:].bitcast(I32), 0)
            for q in range(QUADRANTS):
                nc.sync.dma_start(
                    planes[32 * q : 32 * q + 8, :].bitcast(I32),
                    table_scales[table].bitcast(I32)[:, 4 * q : 4 * q + 4, :],
                )
            loaded[table + "_sc"] = planes

        def load_words(name, dram, a, width):
            words = sbuf([P, width], U32, name)
            nc.sync.dma_start(
                words[:].bitcast(I32), dram[a].rearrange("p n i -> p (n i)").bitcast(I32)
            )
            loaded[name] = words

        def load_table_words(table, b):
            load_words("%s_%d" % (table, b), table_words[table], b, T3)

        def load_w1(b, a):
            raw = sbuf([P, PACK, PASS], F32, "w1_raw_%d_%d" % (b, a))
            rows = w1[a * PASS : (a + 1) * PASS, b * PASS : (b + 1) * PASS]
            nc.sync.dma_start(raw[:], rows.rearrange("(p i) c -> p i c", i=PACK))
            loaded["w1", b, a] = raw

        def load_w2():
            words = sbuf([P, NPASS, H], U16, "w2")
            nc.sync.dma_start(
                words[:].bitcast(I32), w2_words.bitcast(I32).rearrange("a p c -> p a c")
            )
            loaded["w2"] = words

        def load_gain():
            tile = sbuf([P, NPASS, PACK], F32, "gain")
            nc.sync.dma_start(tile[:], gain.rearrange("(b p t) -> p b t", b=NPASS, t=PACK))
            loaded["gain"] = tile

        def load_least():
            tile = sbuf([P, S2 // P], F32, "least")
            with nc.allow_non_contiguous_dma(reason="one value of least for each partition"):
                nc.sync.dma_start(tile[:], least.rearrange("(mt p) -> p mt", p=P))
            loaded["least"] = tile

        w1_bf, w1_codes, w1_plane, w2_codes, w2_plane = {}, {}, {}, {}, {}

        def cast_w1(b, a):
            grouped = sbuf([P, PACK, P, PACK], BF16, "w1_bf_%d_%d" % (b, a))
            source = loaded["w1", b, a][:].rearrange("p i (m t) -> p m i t", t=PACK)
            for tp in range(2):
                nc.scalar.copy(
                    out=grouped[:, 2 * tp : 2 * tp + 2].rearrange("p t m i -> p m i t"),
                    in_=source[:, :, :, 2 * tp : 2 * tp + 2],
                )
            w1_bf[b, a] = grouped

        def quantize_w1(b, a):
            codes = sbuf([P, PASS], U32, "w1_codes_%d_%d" % (b, a))
            plane = sbuf([P, PASS], U8, "w1_plane_%d_%d" % (b, a))
            nc.vector.quantize_mx(
                out=codes[:].bitcast(E4M3),
                scales=plane[:],
                in_=w1_bf[b, a][:].rearrange("p t m i -> p (t m i)"),
            )
            w1_codes[b, a], w1_plane[b, a] = codes, plane

        def reorder_columns(b, raw, dtype, name):
            ordered = sbuf([P, NPASS, PASS], dtype, name)
            nc.vector.tensor_copy(
                out=ordered[:].rearrange("p a (t m) -> p a t m", t=PACK),
                in_=raw[:, :, b * PASS : (b + 1) * PASS].rearrange("p a (m t) -> p a t m", t=PACK),
            )
            return ordered

        def reorder_w2_codes(b):
            w2_codes[b] = reorder_columns(b, loaded["w2"], U16, "w2_codes_%d" % b)

        def reorder_w2_plane(b):
            w2_plane[b] = reorder_columns(b, loaded["w2_sc"], U8, "w2_plane_%d" % b)

        g_words = {}
        g_plane = [sbuf([P, S], U8, "g_plane_%d" % a) for a in range(NPASS)]
        picked_words, picked_planes = {}, {}

        def gather(dst, window, offsets):
            nc.vector.tensor_copy(dst, window.indirect(offsets))

        def gather_table_words(table, b):
            picked = sbuf([P, S2], U32, "picked_%s_%d" % (table, b))
            gather(picked[:], loaded["%s_%d" % (table, b)][:], lists[table][:])
            picked_words[table, b] = picked

        def gather_table_planes(table):
            picked = sbuf([P, S2], U8, "picked_%s_sc" % table)
            gather(picked[:], loaded[table + "_sc"][:], lists[table][:])
            picked_planes[table] = picked

        angle_ps, plain_ps, turns, reduced, wave = {}, {}, {}, {}, {}
        h_rows, h_bf, h_codes, h_plane = {}, {}, {}, {}

        def angle_product(i):
            b, jh, tp = STEPS[i]
            cols = slice(jh * HALF, (jh + 1) * HALF)
            bank = psum.tile([P, 2, HALF], F32, name="bank")
            for a in range(NPASS):
                for u in range(2):
                    m = slice((2 * tp + u) * P, (2 * tp + u + 1) * P)
                    nc.tensor.matmul_mx(
                        out=bank[:, u, :],
                        lhsT=w1_codes[b, a][:, m].bitcast(E4M3), lhsT_scale=w1_plane[b, a][:, m],
                        rhs=g_words[a][:, cols].bitcast(E4M3), rhs_scale=g_plane[a][:, cols],
                        start=(a == 0 and u == 0), stop=(a == NPASS - 1 and u == 1),
                    )
            angle_ps[i] = bank

        def plain_product(i):
            b, jh, tp = STEPS[i]
            cols = slice(jh * HALF, (jh + 1) * HALF)
            bank = psum.tile([P, 2, HALF], F32, name="bank")
            for u in range(2):
                m = slice((2 * tp + u) * P, (2 * tp + u + 1) * P)
                for a in range(NPASS):
                    nc.tensor.matmul_mx(
                        out=bank[:, u, :],
                        lhsT=w2_codes[b][:, a, m].bitcast(E2M1), lhsT_scale=w2_plane[b][:, a, m],
                        rhs=g_words[a][:, cols].bitcast(E4M3), rhs_scale=g_plane[a][:, cols],
                        start=(a == 0), stop=(a == NPASS - 1),
                    )
            plain_ps[i] = bank

        def count_turns(i):
            x = angle_ps[i][:].rearrange("p u j -> p (u j)")
            if i in TURNS_ON_VECTOR:
                n = sbuf([P, 2 * HALF], I32, "turns_%d" % i)
                nc.vector.tensor_scalar(n[:], x, 1.0 / TWO_PI, None, ALU.mult)
                turns[i] = n
            else:
                n = sbuf([P, 2 * HALF], U32, "turns_%d" % i)
                nc.scalar.activation(n[:], x, ACT.Copy, bias=TURN_OFFSET, scale=1.0 / TWO_PI)
                back = sbuf([P, 2 * HALF], F32, "back_%d" % i)
                nc.scalar.activation(
                    back[:], n[:], ACT.Copy, bias=TURN_OFFSET * TWO_PI, scale=-TWO_PI
                )
                turns[i] = back

        def reduce_angle(i):
            x = angle_ps[i][:].rearrange("p u j -> p (u j)")
            y = sbuf([P, 2 * HALF], F32, "reduced_%d" % i)
            if i in TURNS_ON_VECTOR:
                nc.vector.scalar_tensor_tensor(y[:], turns[i][:], -TWO_PI, x, ALU.mult, ALU.add)
            else:
                nc.vector.tensor_tensor(y[:], x, turns[i][:], ALU.add)
            reduced[i] = y

        def sine(i):
            s = sbuf([P, 2, HALF], F32, "wave_%d" % i)
            nc.scalar.activation(s[:].rearrange("p u j -> p (u j)"), reduced[i][:], ACT.Sin)
            wave[i] = s

        def combine(i):
            b, jh, tp = STEPS[i]
            if tp == 0:
                h_rows[b, jh] = sbuf([P, PACK, HALF], BF16, "h_rows_%d_%d" % (b, jh))
            for u in range(2):
                t = 2 * tp + u
                nc.vector.scalar_tensor_tensor(
                    h_rows[b, jh][:, t, :], wave[i][:, u, :], loaded["gain"][:, b, t : t + 1],
                    plain_ps[i][:, u, :], ALU.mult, ALU.add,
                )

        def interleave_h(b, jh, copy):
            grouped = sbuf([P, HALF, PACK], BF16, "h_bf_%d_%d" % (b, jh))
            copy(
                out=grouped[:].rearrange("p (c i) t -> p c t i", i=4),
                in_=h_rows[b, jh][:].rearrange("p t (c i) -> p c t i", i=4),
            )
            h_bf[b, jh] = grouped

        def quantize_h(b, jh):
            codes = sbuf([P, HALF], U32, "h_codes_%d_%d" % (b, jh))
            plane = sbuf([P, HALF], U8, "h_plane_%d_%d" % (b, jh))
            nc.vector.quantize_mx(
                out=codes[:].bitcast(E4M3), scales=plane[:],
                in_=h_bf[b, jh][:].rearrange("p j t -> p (j t)"),
            )
            h_codes[b, jh], h_plane[b, jh] = codes, plane

        score_ps = {}

        def score_pass(jh, b):
            for mp in range(2):
                for table in ("v3", "v2"):
                    if b == 0:
                        score_ps[jh, mp, table] = psum.tile([P, 2, HALF], F32, name="bank")
                    bank = score_ps[jh, mp, table]
                    for u in range(2):
                        m = slice((2 * mp + u) * P, (2 * mp + u + 1) * P)
                        nc.tensor.matmul_mx(
                            out=bank[:, u, :],
                            lhsT=picked_words[table, b][:, m].bitcast(E4M3),
                            lhsT_scale=picked_planes[table][4 * b : P, m],
                            rhs=h_codes[b, jh][:].bitcast(E4M3), rhs_scale=h_plane[b, jh][:],
                            start=(b == 0 and u == 0), stop=(b == NPASS - 1 and u == 1),
                        )

        out_view = out.rearrange("(mt p) j -> p mt j", p=P)

        def finish(jh):
            for mp in range(2):
                limit = limits.tile([P, 2, HALF], F32, name="limit")
                nc.scalar.copy(out=limit[:], in_=score_ps[jh, mp, "v3"][:])
                res = sbuf([P, 2, HALF], F32, "res_%d_%d" % (jh, mp))
                for u in range(2):
                    mt = 2 * mp + u
                    nc.vector.scalar_tensor_tensor(
                        res[:, u, :], score_ps[jh, mp, "v2"][:, u, :],
                        loaded["least"][:, mt : mt + 1], limit[:, u, :], ALU.max, ALU.min,
                    )
                nc.sync.dma_start(
                    out_view[:, 2 * mp : 2 * mp + 2, jh * HALF : (jh + 1) * HALF], res[:]
                )

        load_w1(0, 0)
        load_w1(0, 1)
        for a in range(NPASS):
            load_words("v_words_%d" % a, tab_words, a, T)
        load_planes_side_by_side(v_sc, tab_scales)
        warm_in = sbuf([P, 1], F32, "warm_in")
        nc.vector.memset(warm_in[:], 0.0)
        warm_out = sbuf([P, 1], F32, "warm_out")
        nc.scalar.activation(warm_out[:], warm_in[:], ACT.Sin)
        for a in range(NPASS):
            gather(g_plane[a][:], v_sc[:, a, :], idx[:])
        cast_w1(0, 0)
        load_w2()
        cast_w1(0, 1)
        load_w2_scales()
        load_w1(1, 0)
        quantize_w1(0, 0)
        load_gain()
        g_words[0] = sbuf([P, S], U32, "g_words_0")
        gather(g_words[0][:], loaded["v_words_0"][:], idx[:])
        load_w1(1, 1)
        quantize_w1(0, 1)
        g_words[1] = sbuf([P, S], U32, "g_words_1")
        for jh in range(2):
            gather(
                g_words[1][:, jh * HALF : (jh + 1) * HALF], loaded["v_words_1"][:],
                idx[:, jh * LIST_HALF : (jh + 1) * LIST_HALF],
            )
        for b in range(NPASS):
            load_table_words("v3", b)
        reorder_w2_plane(0)
        reorder_w2_codes(0)

        def prepare_second_group(a):
            cast_w1(1, a)
            load_table_scales(("v3", "v2")[a])
            quantize_w1(1, a)

        late_gathers = {
            1: [lambda: gather_table_words("v3", 0)],
            2: [lambda: gather_table_words("v3", 1)],
            3: [lambda: gather_table_planes("v3")],
            4: [lambda: gather_table_words("v2", 0)],
            5: [lambda: gather_table_words("v2", 1), lambda: gather_table_planes("v2")],
        }

        for i in range(STEPS_IN_PSUM):
            angle_product(i)
        for i in range(STEPS_IN_PSUM):
            plain_product(i)
        for i in range(LOOKAHEAD):
            count_turns(i)
        for i in range(len(STEPS)):
            reduce_angle(i)
            sine(i)
            if i >= 1:
                combine(i - 1)
            if i == 0:
                reorder_w2_codes(1)
                load_table_words("v2", 0)
                reorder_w2_plane(1)
                load_table_words("v2", 1)
                prepare_second_group(0)
                load_least()
            elif i == 1:
                prepare_second_group(1)
            elif i % 2 == 0:
                interleave_h(*STEPS[i - 1][:2], nc.scalar.copy)
            else:
                quantize_h(*STEPS[i - 2][:2])
            for job in late_gathers.get(i, []):
                job()
            ahead = i + LOOKAHEAD
            if ahead < len(STEPS):
                if ahead >= STEPS_IN_PSUM:
                    angle_product(ahead)
                    plain_product(ahead)
                count_turns(ahead)
        combine(len(STEPS) - 1)

        score_pass(0, 0)
        score_pass(0, 1)
        interleave_h(1, 1, nc.vector.tensor_copy)
        score_pass(1, 0)
        finish(0)
        quantize_h(1, 1)
        score_pass(1, 1)
        finish(1)
